import numpy as np
import ml_dtypes


def mxq(x, axis, fmt="e4m3"):
    dtype, down = {"e4m3": (ml_dtypes.float8_e4m3fn, 7), "e5m2": (ml_dtypes.float8_e5m2, 14)}[fmt]
    v = np.moveaxis(np.asarray(x, np.float32).astype(ml_dtypes.bfloat16).astype(np.float64), axis, -1)
    blocks = v.reshape(v.shape[:-1] + (-1, 32))
    amax = np.abs(blocks).max(-1, keepdims=True)
    byte = np.maximum(np.where(amax > 0, np.frexp(amax)[1] - 1 + 127, 0) - down, 1)
    scale = np.exp2(byte - 127.0)
    codes = (blocks / scale).astype(np.float32).astype(dtype).astype(np.float64)
    return np.moveaxis((codes * scale).reshape(v.shape), -1, axis)


WIDE = False


def mx_kscale(k):
    if not WIDE:
        return np.ones(k)
    levels = np.array([10, -10, 5, -5, 0])
    if k % 512:
        return np.exp2(np.random.permutation(np.resize(levels, k // 32))).repeat(32)
    a = np.empty((k // 512, 16))
    for p in range(k // 512):
        a[p, :8] = np.random.permutation(np.resize(levels, 8))
        for g in range(8):
            far = levels[np.abs(levels - a[p, g]) >= 10]
            a[p, g + 8] = far[np.random.randint(len(far))]
    return np.exp2(a.ravel()).repeat(32)


def f64(x):
    return np.asarray(x).astype(np.float64)


def striped(idx):
    return np.tile(idx.reshape(-1, 16).T, (8, 1)).astype(np.uint16)


def unstriped(offs):
    return offs[:16].T.reshape(-1).astype(np.int64)


def striped8(idx):
    return np.concatenate([x.reshape(-1, 16).T for x in idx]).astype(np.uint16)


def runs(offs, k):
    lists = np.stack([offs[16 * r : 16 * r + 16].T.reshape(-1) for r in range(8)]).astype(np.int64)
    return lists[np.arange(k) % 512 // 64]


def pack_weight(w):
    k, n = w.shape
    w = f64(np.asarray(w, np.float32).astype(ml_dtypes.bfloat16)).reshape(k // 32, 32, n)
    amax = np.abs(w).max(1)
    byte = np.clip(np.where(amax > 0, np.frexp(amax)[1] - 1 + 127 - 7, 1), 1, 254)
    scaled = (w * np.exp2(127.0 - byte)[:, None, :]).reshape(k, n).astype(np.float32)
    words = np.ascontiguousarray(scaled.reshape(k // 512, 128, 4, n).transpose(0, 1, 3, 2)).astype(ml_dtypes.float8_e4m3fn).view(np.uint8)
    return words, np.ascontiguousarray(byte.astype(np.uint8).reshape(k // 512, 16, n))


def unpack_weight(words, scales):
    g, p, n, _ = words.shape
    vals = np.ascontiguousarray(words).view(ml_dtypes.float8_e4m3fn).astype(np.float64) * np.repeat(np.exp2(scales.astype(np.float64) - 127.0), 8, axis=1)[..., None]
    return vals.transpose(0, 1, 3, 2).reshape(g * 512, n)


E2M1 = np.array([0.0, 0.5, 1.0, 1.5, 2.0, 3.0, 4.0, 6.0, -0.0, -0.5, -1.0, -1.5, -2.0, -3.0, -4.0, -6.0])


def pack_fp4(w):
    k, n = w.shape
    w = f64(np.asarray(w, np.float32).astype(ml_dtypes.bfloat16)).reshape(k // 32, 32, n)
    amax = np.abs(w).max(1)
    mant, ex = np.frexp(amax / 6.0)
    byte = np.clip(np.where(amax > 0, np.where(mant > 0.5, ex, ex - 1) + 127, 1), 1, 254)
    scaled = (w * np.exp2(127.0 - byte)[:, None, :]).reshape(k, n).astype(np.float32)
    c = np.ascontiguousarray(scaled.reshape(k // 512, 128, 4, n).transpose(0, 1, 3, 2)).astype(ml_dtypes.float4_e2m1fn).view(np.uint8) & 0xF
    words = (c[..., 0::2] | (c[..., 1::2] << 4)).reshape(k // 512, 128, 2 * n)
    return np.ascontiguousarray(words), np.ascontiguousarray(byte.astype(np.uint8).reshape(k // 512, 16, n))


def unpack_fp4(words, scales):
    g, _, n = scales.shape
    words = np.ascontiguousarray(words).reshape(g, 128, n, 2)
    nib = np.empty((g, 128, n, 4), np.uint8)
    nib[..., 0::2] = words & 0xF
    nib[..., 1::2] = words >> 4
    vals = E2M1[nib] * np.repeat(np.exp2(scales.astype(np.float64) - 127.0), 8, axis=1)[..., None]
    return vals.transpose(0, 1, 3, 2).reshape(g * 512, n)


K, T, S, N, G, H, W = 512, 1024, 512, 512, 2048, 512, 256


def setup_inputs():
    n = np.random.standard_normal
    s = mx_kscale(K)[:, None]
    u = mx_kscale(S)
    packed_xT = pack_weight(n((K, T)) * s)
    packed_dT = pack_weight(n((K, G)) / s)
    packed_w1 = pack_fp4(n((H, N)) / np.sqrt(H) / u[:, None])
    perm = np.stack([np.random.permutation(S) for _ in range(8)])
    return {
        "x_words": packed_xT[0],
        "x_scales": packed_xT[1],
        "d_words": packed_dT[0],
        "d_scales": packed_dT[1],
        "gn": (np.random.uniform(0.5, 1.5, (H, 1)) * u[:, None]).astype(np.float32),
        "w1_words": packed_w1[0],
        "w1_scales": packed_w1[1],
        "offs": striped(np.random.permutation(T)[:S]),
        "ka": striped8(np.random.randint(0, G, (8, H))),
        "kb": striped8(np.random.randint(0, G, (8, H))),
        "n1": striped8(perm[:, :W]),
        "n2": striped8(perm[:, W:]),
    }


def reference(x_words, x_scales, d_words, d_scales, gn, w1_words, w1_scales, offs, ka, kb, n1, n2):
    d_ka = unpack_weight(d_words, d_scales)[np.arange(K)[:, None], runs(ka, K)]
    xq = unpack_weight(x_words, x_scales)[:, unstriped(offs)]
    d_kb = unpack_weight(d_words, d_scales)[np.arange(K)[:, None], runs(kb, K)]
    h = 0.0625 * (d_ka.T @ xq + d_kb.T @ xq)
    z = f64(gn) * h
    h2 = unpack_fp4(w1_words, w1_scales).T @ mxq(z, 0, "e4m3")
    pa = h2[np.arange(N)[:, None], runs(n1, N)]
    pb = h2[np.arange(N)[:, None], runs(n2, N)]
    ra = np.maximum(pa, pb)
    out = h2.copy()
    out[np.arange(N)[:, None], runs(n1, N)] = ra
    return out

@@ -1,0 +1,210 @@
+from contextlib import ExitStack
+
+import concourse.mybir as mybir
+from concourse.masks import make_identity
+
+K, T, S, N, G, H, W = 512, 1024, 512, 512, 2048, 512, 256
+FLOPS = 2 * K * H * S * 2 + 2 * H * N * S
+
+F32 = mybir.dt.float32
+BF16 = mybir.dt.bfloat16
+I32 = mybir.dt.int32
+U32 = mybir.dt.uint32
+U16 = mybir.dt.uint16
+U8 = mybir.dt.uint8
+FP8X4 = mybir.dt.float8_e4m3fn_x4
+FP4X4 = mybir.dt.float4_e2m1fn_x4
+COPY = mybir.ActivationFunctionType.Copy
+MULT = mybir.AluOpType.mult
+MAX = mybir.AluOpType.max
+
+P = 128
+PACK = 4
+CHUNKS = S // P
+HALF = S // 2
+LIST_COLS = P // 16
+
+
+def tile_picked_aqlifill_none_p_kernel(
+    tc, x_words, x_scales, d_words, d_scales, gn, w1_words, w1_scales, offs, ka, kb, n1, n2, out
+):
+    nc = tc.nc
+    with ExitStack() as ctx:
+        keep = ctx.enter_context(tc.tile_pool(name="keep", bufs=1))
+        psum = ctx.enter_context(tc.psum_pool(name="psum", bufs=1))
+
+        ka_t = keep.tile([P, H // 16], U16, name="ka_t")
+        kb_t = keep.tile([P, H // 16], U16, name="kb_t")
+        offs_t = keep.tile([P, S // 16], U16, name="offs_t")
+        n1_t = keep.tile([P, W // 16], U16, name="n1_t")
+        n2_t = keep.tile([P, W // 16], U16, name="n2_t")
+
+        d_tab = keep.tile([P, G], U32, name="d_tab", tag="codewords", align_bytes=64)
+        x_tab = keep.tile([P, T], U32, name="x_tab", align_bytes=64)
+        ds_tab = keep.tile([P, G], U8, name="ds_tab", align_bytes=64)
+        xs_tab = keep.tile([P, T], U8, name="xs_tab", tag="scale_rows", align_bytes=64)
+        planes = keep.tile([P, 2 * H + S], U8, name="planes", align_bytes=64)
+        ident = keep.tile([P, P], F32, name="ident")
+
+        nc.vector.memset(ds_tab[:].bitcast(I32), 0)
+        nc.vector.memset(xs_tab[:].bitcast(I32), 0)
+        nc.vector.memset(planes[:].bitcast(I32), 0)
+        nc.vector.memset(ident[:], 0.0)
+        make_identity(nc, ident[:], nomemset=True)
+
+        nc.sync.dma_start(ka_t[:], ka)
+        nc.sync.dma_start(kb_t[:], kb)
+        for a in range(2):
+            nc.sync.dma_start(ds_tab[a:P:16, :].bitcast(I32), d_scales[0][a:16:2, :].bitcast(I32))
+        nc.sync.dma_start(offs_t[:], offs)
+        for a in range(2):
+            nc.sync.dma_start(xs_tab[a:P:16, :].bitcast(I32), x_scales[0][a:16:2, :].bitcast(I32))
+        nc.sync.dma_start(x_tab[:].bitcast(I32), x_words[0].rearrange("p n t -> p (n t)").bitcast(I32))
+        nc.sync.dma_start(d_tab[:].bitcast(I32), d_words[0].rearrange("p n t -> p (n t)").bitcast(I32))
+        gn_t = keep.tile([P, PACK], F32, name="gn_t")
+        nc.gpsimd.dma_start(gn_t[:], gn.rearrange("(p b) o -> p (b o)", b=PACK))
+        w_raw = keep.tile([P, 2 * N], U8, name="w_raw", align_bytes=64)
+        nc.sync.dma_start(w_raw[:].bitcast(I32), w1_words[0].bitcast(I32))
+        nc.sync.dma_start(n2_t[:], n2)
+        nc.sync.dma_start(n1_t[:], n1)
+
+        got = keep.tile([P, 2 * H + S], U8, name="got", align_bytes=64)
+        nc.vector.tensor_copy(got[:, 0:H], ds_tab[:].indirect(ka_t[:]))
+        nc.vector.tensor_copy(got[:, H : 2 * H], ds_tab[:].indirect(kb_t[:]))
+        nc.vector.tensor_copy(got[:, 2 * H : 2 * H + S], xs_tab[:].indirect(offs_t[:]))
+        for r in range(4):
+            src = 16 * (r // 2) + r % 2
+            nc.sync.dma_start(planes[r:P:32, :].bitcast(I32), got[src:P:32, :].bitcast(I32))
+
+        ws_raw = keep.tile([P, N], U8, name="ws_raw", tag="scale_rows", align_bytes=64)
+        nc.gpsimd.memset(ws_raw[:].bitcast(I32), 0)
+        for r in range(4):
+            nc.sync.dma_start(ws_raw[r:P:32, :].bitcast(I32), w1_scales[0][r:16:4, :].bitcast(I32))
+        w_codes = keep.tile([P, 2 * N], U8, name="w_codes", align_bytes=64)
+        w_plane = keep.tile([P, N], U8, name="w_plane", align_bytes=64)
+        nc.scalar.copy(
+            w_codes[:].bitcast(U16).rearrange("p (t m) -> p t m", t=PACK),
+            w_raw[:].bitcast(U16).rearrange("p (m t) -> p t m", t=PACK),
+        )
+        nc.gpsimd.tensor_copy(
+            w_plane[:].rearrange("p (t m) -> p t m", t=PACK),
+            ws_raw[:].rearrange("p (m t) -> p t m", t=PACK),
+        )
+
+        gain_bank = psum.tile([P, PACK, P], F32, name="gain_bank", tag="first0")
+        for b in range(PACK):
+            nc.tensor.transpose(gain_bank[:, b, :], gn_t[:, b : b + 1].to_broadcast([P, P]), ident[:])
+        gain = keep.tile([P, H], F32, name="gain")
+        nc.scalar.activation(
+            gain[:].rearrange("q (u p e) -> q u p e", u=2, e=2),
+            gain_bank[:].rearrange("q (u e) p -> q u p e", u=2),
+            COPY,
+            scale=0.0625,
+        )
+
+        da = keep.tile([P, H], U32, name="da", align_bytes=64)
+        db = keep.tile([P, H], U32, name="db", align_bytes=64)
+        xq_early = keep.tile([P, HALF], U32, name="xq_early", align_bytes=64)
+        h_banks = [psum.tile([P, H], F32, name=f"h_bank{c}", tag=f"h{c}") for c in range(CHUNKS)]
+
+        def pick_tokens(c, xq):
+            nc.vector.tensor_copy(
+                xq[:, c % 2 * P : (c % 2 + 1) * P], x_tab[:].indirect(offs_t[:, c * LIST_COLS : (c + 1) * LIST_COLS])
+            )
+
+        def first_product(c, xq, which):
+            nc.tensor.matmul_mx(
+                out=h_banks[c][:],
+                lhsT=xq[:, c % 2 * P : (c % 2 + 1) * P].bitcast(FP8X4),
+                lhsT_scale=planes[:, 2 * H + c * P : 2 * H + (c + 1) * P],
+                rhs=(da, db)[which][:].bitcast(FP8X4),
+                rhs_scale=planes[:, which * H : (which + 1) * H],
+                start=(which == 0),
+                stop=(which == 1),
+            )
+
+        pick_tokens(0, xq_early)
+        pick_tokens(1, xq_early)
+        nc.vector.tensor_copy(da[:], d_tab[:].indirect(ka_t[:]))
+        first_product(0, xq_early, 0)
+        first_product(1, xq_early, 0)
+        nc.vector.tensor_copy(db[:], d_tab[:].indirect(kb_t[:]))
+        first_product(0, xq_early, 1)
+        first_product(1, xq_early, 1)
+        xq_late = keep.tile([P, HALF], U32, name="xq_late", tag="codewords", align_bytes=64)
+        for c in range(2, CHUNKS):
+            pick_tokens(c, xq_late)
+            first_product(c, xq_late, 0)
+            first_product(c, xq_late, 1)
+
+        zq = keep.tile([P, S], U32, name="zq", align_bytes=64)
+        zq_plane = keep.tile([P, S], U8, name="zq_plane", align_bytes=64)
+        z_rows = [keep.tile([P, H], BF16, name=f"z_rows{c}", align_bytes=64) for c in range(CHUNKS)]
+        z_in = [keep.tile([P, P * PACK], BF16, name=f"z_in{c}", align_bytes=64) for c in range(CHUNKS)]
+
+        def scale_and_turn(c):
+            nc.vector.tensor_tensor(
+                z_rows[c][:].rearrange("q (u p e) -> q u p e", u=2, e=2),
+                h_banks[c][:].rearrange("q (p u e) -> q u p e", u=2, e=2),
+                gain[:].rearrange("q (u p e) -> q u p e", u=2, e=2),
+                MULT,
+            )
+            turned = psum.tile([P, 2, P], F32, name=f"turned{c}", tag=f"turn{c % 2}")
+            words = z_rows[c][:].bitcast(F32)
+            for u in range(2):
+                nc.tensor.transpose(turned[:, u, :], words[:, u * P : (u + 1) * P], ident[:])
+            nc.scalar.copy(
+                z_in[c][:].bitcast(F32).rearrange("p (r u) -> p r u", u=2),
+                turned[:].rearrange("p u r -> p r u"),
+            )
+
+        def quantise(c):
+            cols = slice(c * P, (c + 1) * P)
+            nc.vector.quantize_mx(out=zq[:, cols].bitcast(FP8X4), scales=zq_plane[:, cols], in_=z_in[c][:])
+
+        rows = [keep.tile([P, S], F32, name=f"rows{t}") for t in range(PACK)]
+
+        def second_product(t, half, bank):
+            cols = slice(half * HALF, (half + 1) * HALF)
+            nc.tensor.matmul_mx(
+                out=bank,
+                lhsT=w_codes[:, 2 * t * P : 2 * (t + 1) * P].bitcast(FP4X4),
+                lhsT_scale=w_plane[:, t * P : (t + 1) * P],
+                rhs=zq[:, cols].bitcast(FP8X4),
+                rhs_scale=zq_plane[:, cols],
+                start=True,
+                stop=True,
+            )
+
+        for c in range(CHUNKS):
+            scale_and_turn(c)
+        quantise(0)
+        quantise(1)
+        for pair in range(2):
+            bank = psum.tile([P, 2, HALF], F32, name=f"first{pair}", tag=f"first{pair}")
+            for e in range(2):
+                second_product(2 * pair + e, 0, bank[:, e, :])
+            for e in range(2):
+                nc.scalar.copy(rows[2 * pair + e][:, 0:HALF], bank[:, e, :])
+        quantise(2)
+        quantise(3)
+
+        out_rows = out.rearrange("(p t) j -> t p j", t=PACK)
+        for t in range(PACK):
+            bank = psum.tile([P, HALF], F32, name=f"second{t}", tag=f"h{t}")
+            second_product(t, 1, bank[:])
+            if t == 0:
+                nc.vector.tensor_copy(rows[t][:, HALF:S], bank[:])
+            else:
+                nc.scalar.copy(rows[t][:, HALF:S], bank[:])
+            pa = keep.tile([P, W], F32, name=f"pa{t}", tag="pa")
+            pb = keep.tile([P, W], F32, name=f"pb{t}")
+            ra = keep.tile([P, W], F32, name=f"ra{t}")
+            nc.scalar.activation(pb[:], rows[t][:].indirect(n2_t[:]), COPY)
+            if t == 0:
+                nc.vector.tensor_copy(pa[:], rows[t][:].indirect(n1_t[:]))
+            else:
+                nc.scalar.activation(pa[:], rows[t][:].indirect(n1_t[:]), COPY)
+            nc.vector.tensor_tensor(ra[:], pa[:], pb[:], MAX)
+            nc.vector.tensor_copy(rows[t][:].indirect(n1_t[:]), ra[:])
+            nc.sync.dma_start(out_rows[t], rows[t][:])

@@ -39,28 +39,30 @@ def tile_picked_aqlifill_none_p_kernel(
         n1_t = keep.tile([P, W // 16], U16, name="n1_t")
         n2_t = keep.tile([P, W // 16], U16, name="n2_t")
 
-        d_tab = keep.tile([P, G], U32, name="d_tab", tag="codewords", align_bytes=64)
+        d_tab = keep.tile([P, G], U32, name="d_tab", align_bytes=64)
         x_tab = keep.tile([P, T], U32, name="x_tab", align_bytes=64)
-        ds_tab = keep.tile([P, G], U8, name="ds_tab", align_bytes=64)
-        xs_tab = keep.tile([P, T], U8, name="xs_tab", tag="scale_rows", align_bytes=64)
-        planes = keep.tile([P, 2 * H + S], U8, name="planes", align_bytes=64)
+        ds_tab = keep.tile([P, G], U8, name="ds_tab", tag="scale_rows", align_bytes=64)
+        xs_tab = keep.tile([P, T], U8, name="xs_tab", align_bytes=64)
+        planes_a = keep.tile([P, S + H], U8, name="planes_a", align_bytes=64)
+        planes_b = keep.tile([P, H], U8, name="planes_b", align_bytes=64)
         ident = keep.tile([P, P], F32, name="ident")
 
+        nc.gpsimd.memset(xs_tab[:].bitcast(I32), 0)
         nc.vector.memset(ds_tab[:].bitcast(I32), 0)
-        nc.vector.memset(xs_tab[:].bitcast(I32), 0)
-        nc.vector.memset(planes[:].bitcast(I32), 0)
+        nc.vector.memset(planes_a[:].bitcast(I32), 0)
+        nc.vector.memset(planes_b[:].bitcast(I32), 0)
         nc.vector.memset(ident[:], 0.0)
         make_identity(nc, ident[:], nomemset=True)
 
-        nc.sync.dma_start(ka_t[:], ka)
-        nc.sync.dma_start(kb_t[:], kb)
-        for a in range(2):
-            nc.sync.dma_start(ds_tab[a:P:16, :].bitcast(I32), d_scales[0][a:16:2, :].bitcast(I32))
         nc.sync.dma_start(offs_t[:], offs)
+        nc.sync.dma_start(ka_t[:], ka)
         for a in range(2):
             nc.sync.dma_start(xs_tab[a:P:16, :].bitcast(I32), x_scales[0][a:16:2, :].bitcast(I32))
-        nc.sync.dma_start(x_tab[:].bitcast(I32), x_words[0].rearrange("p n t -> p (n t)").bitcast(I32))
+        for a in range(2):
+            nc.sync.dma_start(ds_tab[a:P:16, :].bitcast(I32), d_scales[0][a:16:2, :].bitcast(I32))
+        nc.sync.dma_start(kb_t[:], kb)
         nc.sync.dma_start(d_tab[:].bitcast(I32), d_words[0].rearrange("p n t -> p (n t)").bitcast(I32))
+        nc.sync.dma_start(x_tab[:].bitcast(I32), x_words[0].rearrange("p n t -> p (n t)").bitcast(I32))
         gn_t = keep.tile([P, PACK], F32, name="gn_t")
         nc.gpsimd.dma_start(gn_t[:], gn.rearrange("(p b) o -> p (b o)", b=PACK))
         w_raw = keep.tile([P, 2 * N], U8, name="w_raw", align_bytes=64)
@@ -68,13 +70,19 @@ def tile_picked_aqlifill_none_p_kernel(
         nc.sync.dma_start(n2_t[:], n2)
         nc.sync.dma_start(n1_t[:], n1)
 
-        got = keep.tile([P, 2 * H + S], U8, name="got", align_bytes=64)
-        nc.vector.tensor_copy(got[:, 0:H], ds_tab[:].indirect(ka_t[:]))
-        nc.vector.tensor_copy(got[:, H : 2 * H], ds_tab[:].indirect(kb_t[:]))
-        nc.vector.tensor_copy(got[:, 2 * H : 2 * H + S], xs_tab[:].indirect(offs_t[:]))
-        for r in range(4):
-            src = 16 * (r // 2) + r % 2
-            nc.sync.dma_start(planes[r:P:32, :].bitcast(I32), got[src:P:32, :].bitcast(I32))
+        got_a = keep.tile([P, S + H], U8, name="got_a", tag="picked", align_bytes=64)
+        got_b = keep.tile([P, H], U8, name="got_b", tag="picked_late", align_bytes=64)
+
+        def place_rows(planes, got):
+            for r in range(4):
+                src = 16 * (r // 2) + r % 2
+                nc.sync.dma_start(planes[r:P:32, :].bitcast(I32), got[src:P:32, :].bitcast(I32))
+
+        nc.vector.tensor_copy(got_a[:, 0:S], xs_tab[:].indirect(offs_t[:]))
+        nc.vector.tensor_copy(got_a[:, S : S + H], ds_tab[:].indirect(ka_t[:]))
+        place_rows(planes_a, got_a)
+        nc.vector.tensor_copy(got_b[:], ds_tab[:].indirect(kb_t[:]))
+        place_rows(planes_b, got_b)
 
         ws_raw = keep.tile([P, N], U8, name="ws_raw", tag="scale_rows", align_bytes=64)
         nc.gpsimd.memset(ws_raw[:].bitcast(I32), 0)
@@ -103,52 +111,47 @@ def tile_picked_aqlifill_none_p_kernel(
         )
 
         da = keep.tile([P, H], U32, name="da", align_bytes=64)
-        db = keep.tile([P, H], U32, name="db", align_bytes=64)
-        xq_early = keep.tile([P, HALF], U32, name="xq_early", align_bytes=64)
+        xq_early = keep.tile([P, S - P], U32, name="xq_early", align_bytes=64)
         h_banks = [psum.tile([P, H], F32, name=f"h_bank{c}", tag=f"h{c}") for c in range(CHUNKS)]
 
         def pick_tokens(c, xq):
-            nc.vector.tensor_copy(
-                xq[:, c % 2 * P : (c % 2 + 1) * P], x_tab[:].indirect(offs_t[:, c * LIST_COLS : (c + 1) * LIST_COLS])
-            )
+            nc.vector.tensor_copy(xq, x_tab[:].indirect(offs_t[:, c * LIST_COLS : (c + 1) * LIST_COLS]))
 
-        def first_product(c, xq, which):
+        def first_product(c, xq, words, plane, first):
             nc.tensor.matmul_mx(
                 out=h_banks[c][:],
-                lhsT=xq[:, c % 2 * P : (c % 2 + 1) * P].bitcast(FP8X4),
-                lhsT_scale=planes[:, 2 * H + c * P : 2 * H + (c + 1) * P],
-                rhs=(da, db)[which][:].bitcast(FP8X4),
-                rhs_scale=planes[:, which * H : (which + 1) * H],
-                start=(which == 0),
-                stop=(which == 1),
+                lhsT=xq.bitcast(FP8X4),
+                lhsT_scale=planes_a[:, c * P : (c + 1) * P],
+                rhs=words.bitcast(FP8X4),
+                rhs_scale=plane,
+                start=first,
+                stop=not first,
             )
 
-        pick_tokens(0, xq_early)
-        pick_tokens(1, xq_early)
+        last = CHUNKS - 1
         nc.vector.tensor_copy(da[:], d_tab[:].indirect(ka_t[:]))
-        first_product(0, xq_early, 0)
-        first_product(1, xq_early, 0)
+        for c in range(last):
+            pick_tokens(c, xq_early[:, c * P : (c + 1) * P])
+            first_product(c, xq_early[:, c * P : (c + 1) * P], da[:], planes_a[:, S : S + H], True)
+        db = keep.tile([P, H], U32, name="db", tag="picked", align_bytes=64)
         nc.vector.tensor_copy(db[:], d_tab[:].indirect(kb_t[:]))
-        first_product(0, xq_early, 1)
-        first_product(1, xq_early, 1)
-        xq_late = keep.tile([P, HALF], U32, name="xq_late", tag="codewords", align_bytes=64)
-        for c in range(2, CHUNKS):
-            pick_tokens(c, xq_late)
-            first_product(c, xq_late, 0)
-            first_product(c, xq_late, 1)
+        for c in range(last):
+            first_product(c, xq_early[:, c * P : (c + 1) * P], db[:], planes_b[:], False)
 
         zq = keep.tile([P, S], U32, name="zq", align_bytes=64)
         zq_plane = keep.tile([P, S], U8, name="zq_plane", align_bytes=64)
         z_rows = [keep.tile([P, H], BF16, name=f"z_rows{c}", align_bytes=64) for c in range(CHUNKS)]
         z_in = [keep.tile([P, P * PACK], BF16, name=f"z_in{c}", align_bytes=64) for c in range(CHUNKS)]
 
-        def scale_and_turn(c):
+        def apply_gain(c, us):
             nc.vector.tensor_tensor(
-                z_rows[c][:].rearrange("q (u p e) -> q u p e", u=2, e=2),
-                h_banks[c][:].rearrange("q (p u e) -> q u p e", u=2, e=2),
-                gain[:].rearrange("q (u p e) -> q u p e", u=2, e=2),
+                z_rows[c][:].rearrange("q (u p e) -> q u p e", u=2, e=2)[:, us],
+                h_banks[c][:].rearrange("q (p u e) -> q u p e", u=2, e=2)[:, us],
+                gain[:].rearrange("q (u p e) -> q u p e", u=2, e=2)[:, us],
                 MULT,
             )
+
+        def turn(c):
             turned = psum.tile([P, 2, P], F32, name=f"turned{c}", tag=f"turn{c % 2}")
             words = z_rows[c][:].bitcast(F32)
             for u in range(2):
@@ -158,14 +161,18 @@ def tile_picked_aqlifill_none_p_kernel(
                 turned[:].rearrange("p u r -> p r u"),
             )
 
+        xq_last = keep.tile([P, P], U32, name="xq_last", tag="picked_late", align_bytes=64)
+        pick_tokens(last, xq_last[:])
+        first_product(last, xq_last[:], da[:], planes_a[:, S : S + H], True)
+        first_product(last, xq_last[:], db[:], planes_b[:], False)
+
         def quantise(c):
             cols = slice(c * P, (c + 1) * P)
             nc.vector.quantize_mx(out=zq[:, cols].bitcast(FP8X4), scales=zq_plane[:, cols], in_=z_in[c][:])
 
         rows = [keep.tile([P, S], F32, name=f"rows{t}") for t in range(PACK)]
 
-        def second_product(t, half, bank):
-            cols = slice(half * HALF, (half + 1) * HALF)
+        def second_product(t, cols, bank):
             nc.tensor.matmul_mx(
                 out=bank,
                 lhsT=w_codes[:, 2 * t * P : 2 * (t + 1) * P].bitcast(FP4X4),
@@ -176,27 +183,34 @@ def tile_picked_aqlifill_none_p_kernel(
                 stop=True,
             )
 
-        for c in range(CHUNKS):
-            scale_and_turn(c)
+        for c in range(last):
+            apply_gain(c, slice(0, 2))
+            turn(c)
+        for u in range(2):
+            apply_gain(last, slice(u, u + 1))
+        turn(last)
         quantise(0)
         quantise(1)
-        for pair in range(2):
-            bank = psum.tile([P, 2, HALF], F32, name=f"first{pair}", tag=f"first{pair}")
-            for e in range(2):
-                second_product(2 * pair + e, 0, bank[:, e, :])
-            for e in range(2):
-                nc.scalar.copy(rows[2 * pair + e][:, 0:HALF], bank[:, e, :])
+        early = psum.tile([P, 2, HALF], F32, name="early", tag="first0")
+        for t in range(2):
+            second_product(t, slice(0, HALF), early[:, t, :])
+        for t in range(2):
+            nc.scalar.copy(rows[t][:, 0:HALF], early[:, t, :])
         quantise(2)
+        third = psum.tile([P, P], F32, name="third", tag="h2")
+        second_product(0, slice(HALF, HALF + P), third[:])
         quantise(3)
+        nc.vector.tensor_copy(rows[0][:, HALF : HALF + P], third[:])
 
         out_rows = out.rearrange("(p t) j -> t p j", t=PACK)
         for t in range(PACK):
-            bank = psum.tile([P, HALF], F32, name=f"second{t}", tag=f"h{t}")
-            second_product(t, 1, bank[:])
+            cols = slice((S - P, HALF, 0, 0)[t], S)
+            bank = psum.tile([P, cols.stop - cols.start], F32, name=f"second{t}", tag="h1")
+            second_product(t, cols, bank[:])
             if t == 0:
-                nc.vector.tensor_copy(rows[t][:, HALF:S], bank[:])
+                nc.vector.tensor_copy(rows[t][:, cols], bank[:])
             else:
-                nc.scalar.copy(rows[t][:, HALF:S], bank[:])
+                nc.scalar.copy(rows[t][:, cols], bank[:])
             pa = keep.tile([P, W], F32, name=f"pa{t}", tag="pa")
             pb = keep.tile([P, W], F32, name=f"pb{t}")
             ra = keep.tile([P, W], F32, name=f"ra{t}")

@@ -40,15 +40,17 @@ def tile_picked_aqlifill_none_p_kernel(
         n2_t = keep.tile([P, W // 16], U16, name="n2_t")
 
         d_tab = keep.tile([P, G], U32, name="d_tab", align_bytes=64)
-        x_tab = keep.tile([P, T], U32, name="x_tab", align_bytes=64)
+        x_tab = keep.tile([P, T], U32, name="x_tab", tag="tokens", align_bytes=64)
         ds_tab = keep.tile([P, G], U8, name="ds_tab", tag="scale_rows", align_bytes=64)
         xs_tab = keep.tile([P, T], U8, name="xs_tab", align_bytes=64)
         planes_a = keep.tile([P, S + H], U8, name="planes_a", align_bytes=64)
         planes_b = keep.tile([P, H], U8, name="planes_b", align_bytes=64)
+        ws_raw = keep.tile([P, N], U8, name="ws_raw", align_bytes=64)
         ident = keep.tile([P, P], F32, name="ident")
 
-        nc.gpsimd.memset(xs_tab[:].bitcast(I32), 0)
+        nc.vector.memset(xs_tab[:].bitcast(I32), 0)
         nc.vector.memset(ds_tab[:].bitcast(I32), 0)
+        nc.vector.memset(ws_raw[:].bitcast(I32), 0)
         nc.vector.memset(planes_a[:].bitcast(I32), 0)
         nc.vector.memset(planes_b[:].bitcast(I32), 0)
         nc.vector.memset(ident[:], 0.0)
@@ -62,11 +64,11 @@ def tile_picked_aqlifill_none_p_kernel(
             nc.sync.dma_start(ds_tab[a:P:16, :].bitcast(I32), d_scales[0][a:16:2, :].bitcast(I32))
         nc.sync.dma_start(kb_t[:], kb)
         nc.sync.dma_start(d_tab[:].bitcast(I32), d_words[0].rearrange("p n t -> p (n t)").bitcast(I32))
+        for r in range(4):
+            nc.sync.dma_start(ws_raw[r:P:32, :].bitcast(I32), w1_scales[0][r:16:4, :].bitcast(I32))
         nc.sync.dma_start(x_tab[:].bitcast(I32), x_words[0].rearrange("p n t -> p (n t)").bitcast(I32))
         gn_t = keep.tile([P, PACK], F32, name="gn_t")
-        nc.gpsimd.dma_start(gn_t[:], gn.rearrange("(p b) o -> p (b o)", b=PACK))
-        w_raw = keep.tile([P, 2 * N], U8, name="w_raw", align_bytes=64)
-        nc.sync.dma_start(w_raw[:].bitcast(I32), w1_words[0].bitcast(I32))
+        nc.sync.dma_start(gn_t[:], gn.rearrange("(p b) o -> p (b o)", b=PACK))
         nc.sync.dma_start(n2_t[:], n2)
         nc.sync.dma_start(n1_t[:], n1)
 
@@ -84,19 +86,12 @@ def tile_picked_aqlifill_none_p_kernel(
         nc.vector.tensor_copy(got_b[:], ds_tab[:].indirect(kb_t[:]))
         place_rows(planes_b, got_b)
 
-        ws_raw = keep.tile([P, N], U8, name="ws_raw", tag="scale_rows", align_bytes=64)
-        nc.gpsimd.memset(ws_raw[:].bitcast(I32), 0)
-        for r in range(4):
-            nc.sync.dma_start(ws_raw[r:P:32, :].bitcast(I32), w1_scales[0][r:16:4, :].bitcast(I32))
+        w_raw = keep.tile([P, 2 * N], U8, name="w_raw", tag="scale_rows", align_bytes=64)
+        nc.sync.dma_start(w_raw[:].bitcast(I32), w1_words[0].bitcast(I32))
         w_codes = keep.tile([P, 2 * N], U8, name="w_codes", align_bytes=64)
-        w_plane = keep.tile([P, N], U8, name="w_plane", align_bytes=64)
         nc.scalar.copy(
             w_codes[:].bitcast(U16).rearrange("p (t m) -> p t m", t=PACK),
             w_raw[:].bitcast(U16).rearrange("p (m t) -> p t m", t=PACK),
-        )
-        nc.gpsimd.tensor_copy(
-            w_plane[:].rearrange("p (t m) -> p t m", t=PACK),
-            ws_raw[:].rearrange("p (m t) -> p t m", t=PACK),
         )
 
         gain_bank = psum.tile([P, PACK, P], F32, name="gain_bank", tag="first0")
@@ -165,6 +160,11 @@ def tile_picked_aqlifill_none_p_kernel(
         pick_tokens(last, xq_last[:])
         first_product(last, xq_last[:], da[:], planes_a[:, S : S + H], True)
         first_product(last, xq_last[:], db[:], planes_b[:], False)
+        w_plane = keep.tile([P, N], U8, name="w_plane", tag="tokens", align_bytes=64)
+        nc.vector.tensor_copy(
+            w_plane[:].rearrange("p (t c i) -> p c t i", t=PACK, i=16),
+            ws_raw[:].rearrange("p (c i t) -> p c t i", t=PACK, i=16),
+        )
 
         def quantise(c):
             cols = slice(c * P, (c + 1) * P)

from contextlib import ExitStack

import concourse.mybir as mybir
from concourse.masks import make_identity

K, T, S, N, G, H, W = 512, 1024, 512, 512, 2048, 512, 256
FLOPS = 2 * K * H * S * 2 + 2 * H * N * S

F32 = mybir.dt.float32
BF16 = mybir.dt.bfloat16
I32 = mybir.dt.int32
U32 = mybir.dt.uint32
U16 = mybir.dt.uint16
U8 = mybir.dt.uint8
FP8X4 = mybir.dt.float8_e4m3fn_x4
FP4X4 = mybir.dt.float4_e2m1fn_x4
COPY = mybir.ActivationFunctionType.Copy
MULT = mybir.AluOpType.mult
MAX = mybir.AluOpType.max

P = 128
PACK = 4
CHUNKS = S // P
HALF = S // 2
LIST_COLS = P // 16


def tile_picked_aqlifill_none_p_kernel(
    tc, x_words, x_scales, d_words, d_scales, gn, w1_words, w1_scales, offs, ka, kb, n1, n2, out
):
    nc = tc.nc
    with ExitStack() as ctx:
        keep = ctx.enter_context(tc.tile_pool(name="keep", bufs=1))
        psum = ctx.enter_context(tc.psum_pool(name="psum", bufs=1))

        ka_t = keep.tile([P, H // 16], U16, name="ka_t")
        kb_t = keep.tile([P, H // 16], U16, name="kb_t")
        offs_t = keep.tile([P, S // 16], U16, name="offs_t")
        n1_t = keep.tile([P, W // 16], U16, name="n1_t")
        n2_t = keep.tile([P, W // 16], U16, name="n2_t")

        d_tab = keep.tile([P, G], U32, name="d_tab", align_bytes=64)
        x_tab = keep.tile([P, T], U32, name="x_tab", tag="tokens", align_bytes=64)
        ds_tab = keep.tile([P, G], U8, name="ds_tab", tag="scale_rows", align_bytes=64)
        xs_tab = keep.tile([P, T], U8, name="xs_tab", align_bytes=64)
        planes_a = keep.tile([P, S + H], U8, name="planes_a", align_bytes=64)
        planes_b = keep.tile([P, H], U8, name="planes_b", align_bytes=64)
        ws_raw = keep.tile([P, N], U8, name="ws_raw", align_bytes=64)
        ident = keep.tile([P, P], F32, name="ident")

        nc.vector.memset(xs_tab[:].bitcast(I32), 0)
        nc.vector.memset(ds_tab[:].bitcast(I32), 0)
        nc.vector.memset(ws_raw[:].bitcast(I32), 0)
        nc.vector.memset(planes_a[:].bitcast(I32), 0)
        nc.vector.memset(planes_b[:].bitcast(I32), 0)
        nc.vector.memset(ident[:], 0.0)
        make_identity(nc, ident[:], nomemset=True)

        nc.sync.dma_start(offs_t[:], offs)
        nc.sync.dma_start(ka_t[:], ka)
        for a in range(2):
            nc.sync.dma_start(xs_tab[a:P:16, :].bitcast(I32), x_scales[0][a:16:2, :].bitcast(I32))
        for a in range(2):
            nc.sync.dma_start(ds_tab[a:P:16, :].bitcast(I32), d_scales[0][a:16:2, :].bitcast(I32))
        nc.sync.dma_start(kb_t[:], kb)
        nc.sync.dma_start(d_tab[:].bitcast(I32), d_words[0].rearrange("p n t -> p (n t)").bitcast(I32))
        for r in range(4):
            nc.sync.dma_start(ws_raw[r:P:32, :].bitcast(I32), w1_scales[0][r:16:4, :].bitcast(I32))
        nc.sync.dma_start(x_tab[:].bitcast(I32), x_words[0].rearrange("p n t -> p (n t)").bitcast(I32))
        gn_t = keep.tile([P, PACK], F32, name="gn_t")
        nc.sync.dma_start(gn_t[:], gn.rearrange("(p b) o -> p (b o)", b=PACK))
        nc.sync.dma_start(n2_t[:], n2)
        nc.sync.dma_start(n1_t[:], n1)

        got_a = keep.tile([P, S + H], U8, name="got_a", tag="picked", align_bytes=64)
        got_b = keep.tile([P, H], U8, name="got_b", tag="picked_late", align_bytes=64)

        def place_rows(planes, got):
            for r in range(4):
                src = 16 * (r // 2) + r % 2
                nc.sync.dma_start(planes[r:P:32, :].bitcast(I32), got[src:P:32, :].bitcast(I32))

        nc.vector.tensor_copy(got_a[:, 0:S], xs_tab[:].indirect(offs_t[:]))
        nc.vector.tensor_copy(got_a[:, S : S + H], ds_tab[:].indirect(ka_t[:]))
        place_rows(planes_a, got_a)
        nc.vector.tensor_copy(got_b[:], ds_tab[:].indirect(kb_t[:]))
        place_rows(planes_b, got_b)

        w_raw = keep.tile([P, 2 * N], U8, name="w_raw", tag="scale_rows", align_bytes=64)
        nc.sync.dma_start(w_raw[:].bitcast(I32), w1_words[0].bitcast(I32))
        w_codes = keep.tile([P, 2 * N], U8, name="w_codes", align_bytes=64)
        nc.scalar.copy(
            w_codes[:].bitcast(U16).rearrange("p (t m) -> p t m", t=PACK),
            w_raw[:].bitcast(U16).rearrange("p (m t) -> p t m", t=PACK),
        )

        gain_bank = psum.tile([P, PACK, P], F32, name="gain_bank", tag="first0")
        for b in range(PACK):
            nc.tensor.transpose(gain_bank[:, b, :], gn_t[:, b : b + 1].to_broadcast([P, P]), ident[:])
        gain = keep.tile([P, H], F32, name="gain")
        nc.scalar.activation(
            gain[:].rearrange("q (u p e) -> q u p e", u=2, e=2),
            gain_bank[:].rearrange("q (u e) p -> q u p e", u=2),
            COPY,
            scale=0.0625,
        )

        da = keep.tile([P, H], U32, name="da", align_bytes=64)
        xq_early = keep.tile([P, S - P], U32, name="xq_early", align_bytes=64)
        h_banks = [psum.tile([P, H], F32, name=f"h_bank{c}", tag=f"h{c}") for c in range(CHUNKS)]

        def pick_tokens(c, xq):
            nc.vector.tensor_copy(xq, x_tab[:].indirect(offs_t[:, c * LIST_COLS : (c + 1) * LIST_COLS]))

        def first_product(c, xq, words, plane, first):
            nc.tensor.matmul_mx(
                out=h_banks[c][:],
                lhsT=xq.bitcast(FP8X4),
                lhsT_scale=planes_a[:, c * P : (c + 1) * P],
                rhs=words.bitcast(FP8X4),
                rhs_scale=plane,
                start=first,
                stop=not first,
            )

        last = CHUNKS - 1
        nc.vector.tensor_copy(da[:], d_tab[:].indirect(ka_t[:]))
        for c in range(last):
            pick_tokens(c, xq_early[:, c * P : (c + 1) * P])
            first_product(c, xq_early[:, c * P : (c + 1) * P], da[:], planes_a[:, S : S + H], True)
        db = keep.tile([P, H], U32, name="db", tag="picked", align_bytes=64)
        nc.vector.tensor_copy(db[:], d_tab[:].indirect(kb_t[:]))
        for c in range(last):
            first_product(c, xq_early[:, c * P : (c + 1) * P], db[:], planes_b[:], False)

        zq = keep.tile([P, S], U32, name="zq", align_bytes=64)
        zq_plane = keep.tile([P, S], U8, name="zq_plane", align_bytes=64)
        z_rows = [keep.tile([P, H], BF16, name=f"z_rows{c}", align_bytes=64) for c in range(CHUNKS)]
        z_in = [keep.tile([P, P * PACK], BF16, name=f"z_in{c}", align_bytes=64) for c in range(CHUNKS)]

        def apply_gain(c, us):
            nc.vector.tensor_tensor(
                z_rows[c][:].rearrange("q (u p e) -> q u p e", u=2, e=2)[:, us],
                h_banks[c][:].rearrange("q (p u e) -> q u p e", u=2, e=2)[:, us],
                gain[:].rearrange("q (u p e) -> q u p e", u=2, e=2)[:, us],
                MULT,
            )

        def turn(c):
            turned = psum.tile([P, 2, P], F32, name=f"turned{c}", tag=f"turn{c % 2}")
            words = z_rows[c][:].bitcast(F32)
            for u in range(2):
                nc.tensor.transpose(turned[:, u, :], words[:, u * P : (u + 1) * P], ident[:])
            nc.scalar.copy(
                z_in[c][:].bitcast(F32).rearrange("p (r u) -> p r u", u=2),
                turned[:].rearrange("p u r -> p r u"),
            )

        xq_last = keep.tile([P, P], U32, name="xq_last", tag="picked_late", align_bytes=64)
        pick_tokens(last, xq_last[:])
        first_product(last, xq_last[:], da[:], planes_a[:, S : S + H], True)
        first_product(last, xq_last[:], db[:], planes_b[:], False)
        w_plane = keep.tile([P, N], U8, name="w_plane", tag="tokens", align_bytes=64)
        nc.vector.tensor_copy(
            w_plane[:].rearrange("p (t c i) -> p c t i", t=PACK, i=16),
            ws_raw[:].rearrange("p (c i t) -> p c t i", t=PACK, i=16),
        )

        def quantise(c):
            cols = slice(c * P, (c + 1) * P)
            nc.vector.quantize_mx(out=zq[:, cols].bitcast(FP8X4), scales=zq_plane[:, cols], in_=z_in[c][:])

        rows = [keep.tile([P, S], F32, name=f"rows{t}") for t in range(PACK)]

        def second_product(t, cols, bank):
            nc.tensor.matmul_mx(
                out=bank,
                lhsT=w_codes[:, 2 * t * P : 2 * (t + 1) * P].bitcast(FP4X4),
                lhsT_scale=w_plane[:, t * P : (t + 1) * P],
                rhs=zq[:, cols].bitcast(FP8X4),
                rhs_scale=zq_plane[:, cols],
                start=True,
                stop=True,
            )

        for c in range(last):
            apply_gain(c, slice(0, 2))
            turn(c)
        for u in range(2):
            apply_gain(last, slice(u, u + 1))
        turn(last)
        quantise(0)
        quantise(1)
        early = psum.tile([P, 2, HALF], F32, name="early", tag="first0")
        for t in range(2):
            second_product(t, slice(0, HALF), early[:, t, :])
        for t in range(2):
            nc.scalar.copy(rows[t][:, 0:HALF], early[:, t, :])
        quantise(2)
        third = psum.tile([P, P], F32, name="third", tag="h2")
        second_product(0, slice(HALF, HALF + P), third[:])
        quantise(3)
        nc.vector.tensor_copy(rows[0][:, HALF : HALF + P], third[:])

        out_rows = out.rearrange("(p t) j -> t p j", t=PACK)
        for t in range(PACK):
            cols = slice((S - P, HALF, 0, 0)[t], S)
            bank = psum.tile([P, cols.stop - cols.start], F32, name=f"second{t}", tag="h1")
            second_product(t, cols, bank[:])
            if t == 0:
                nc.vector.tensor_copy(rows[t][:, cols], bank[:])
            else:
                nc.scalar.copy(rows[t][:, cols], bank[:])
            pa = keep.tile([P, W], F32, name=f"pa{t}", tag="pa")
            pb = keep.tile([P, W], F32, name=f"pb{t}")
            ra = keep.tile([P, W], F32, name=f"ra{t}")
            nc.scalar.activation(pb[:], rows[t][:].indirect(n2_t[:]), COPY)
            if t == 0:
                nc.vector.tensor_copy(pa[:], rows[t][:].indirect(n1_t[:]))
            else:
                nc.scalar.activation(pa[:], rows[t][:].indirect(n1_t[:]), COPY)
            nc.vector.tensor_tensor(ra[:], pa[:], pb[:], MAX)
            nc.vector.tensor_copy(rows[t][:].indirect(n1_t[:]), ra[:])
            nc.sync.dma_start(out_rows[t], rows[t][:])
